import numpy as np
CORES = [0,1,2,3,4,5,6,7,8,9,10,11,12,13,14,15,16,17,18,19,20,21,22,23,24,25,26,27,28,29,30,31,32,33,34,35,36,37,38,39,40,41,42,43,44,45,46,47,48,49,50,51,52,53,54,55,56,57,58,59,60,61,62,63,64,65,66,67,68,69,70,71,72,73,74,75,76,77,78,79,80,81,82,83,84,85,86,87,88,89,90,91,92,93,94,95,96,97,98,99,100,101,102,103,104,105,106,107,108,109,110,111,112,113,114,115,116,117,118,119,120,121,122,123,124,125,126,127,128,129,130,131,132,133,134,135,136,137,138,139,140,141,142,143,144,145,146,147,148,149,150,151,152,153,154,155,156,157,158,159,160,161,162,163,164,165,166,167,168,169,170,171,172,173,174,175,176,177,178,179,180,181,182,183,184,185,186,187,188,189,190,191,192,193,194,195,196,197,198,199,200,201,202,203,204,205,206,207,208,209,210,211,212,213,214,215,216,217,218,219,220,221,222,223,224,225,226,227,228,229,230,231,232,233,234,235,236,237,238,239,240,241,242,243,244,245,246,247,248,249,250,251,252,253,254,255]
N = 256
DEAD = {"mate_links":[[24,0]],"switch_ports":[[3,0],[3,1],[20,1]],"chips":[]}
def setup_inputs(rng):
    return {"x": rng.standard_normal((N, 128, 256), dtype=np.float32)}
def reference(x):
    s = x.sum(axis=0, dtype=np.float64).astype(x.dtype)
    return {"y": np.broadcast_to(s, (N,) + s.shape)}

@@ -1,0 +1,276 @@
+import comms_topo
+import concourse.bass as bass
+
+N_CORES = 256
+BY_HOST = True
+
+
+def build_plan(dead, by_host):
+    if dead["chips"]:
+        raise ValueError("missing chips are not planned for")
+    dead_ports = set((c, d) for c, d in dead["switch_ports"])
+    dead_mates = set()
+    for c, d in dead["mate_links"]:
+        dead_mates.add((c, d))
+        dead_mates.add((c ^ 1, d))
+    side_die = [comms_topo.die(0), comms_topo.die(4)]
+    chips = list(range(N_CORES // 8))
+
+    def role(gc, t):
+        d = side_die[t]
+        mine, other = (gc, d) not in dead_ports, (gc ^ 1, d) not in dead_ports
+        link = (gc, d) not in dead_mates
+        if mine and other:
+            return "R" if link else "C"
+        if link and (mine or other):
+            return "M" if mine else "L"
+        raise ValueError("chip %d side %d is cut off" % (gc, t))
+
+    def group(gc):
+        return gc // 16 if by_host else 0
+
+    n_groups = 2 if by_host else 1
+
+    def owners(grp, t, p):
+        return [c for c in chips if group(c) == grp and c % 2 == p and role(c, t) == "R"]
+
+    def pieces(n, t, i):
+        base, extra = 32 // n, 32 % n
+        first = (extra * (2 * t + i)) % n
+        out, off = [], 0
+        for j in range(n):
+            w = base + (1 if (j - first) % n < extra else 0)
+            out.append((off, w))
+            off += w
+        return out
+
+    def core(gc, k):
+        return 8 * gc + k
+
+    def a(t, i):
+        return 4 * t + i
+
+    def b(t, i):
+        return 4 * t + 2 + i
+
+    def col(t, p, i):
+        return 128 * t + 64 * p + 32 * i
+
+    CHIP, MATE, PLANE, RELAY, HOST = 1, 2, 3, 4, 5
+    GATHER = 6 if by_host else 5
+    BACK, SPREAD = GATHER + 1, GATHER + 2
+    blocks = [(t, p, i) for t in range(2) for p in range(2) for i in range(2)]
+    ops, top = [], [0] * N_CORES
+
+    def slot(c, w):
+        off = top[c]
+        top[c] += w
+        return off
+
+    def emit(stage, src, srcs, dsts, w):
+        for k in range(0, len(dsts), 16):
+            ops.append((stage, src, tuple(srcs), tuple(dsts[k:k + 16]), w))
+
+    def send(stage, src, srcs, dst, w):
+        off = slot(dst, w)
+        emit(stage, src, srcs, [(dst, "land", off)], w)
+        return ("land", off)
+
+    def cut(bufs, off):
+        return [(n, o + off) for n, o in bufs]
+
+    have = {}
+    for gc in chips:
+        for blk in blocks:
+            t, p, i = blk
+            own = p == gc % 2
+            if role(gc, t) == "L":
+                own = not own
+            h = core(gc, a(t, i) if own else b(t, i))
+            have[(h, blk)] = [("xs", col(*blk))]
+            for k in range(8):
+                if core(gc, k) != h:
+                    have[(h, blk)].append(send(CHIP, core(gc, k), [("xs", col(*blk))], h, 32))
+
+    late = {}
+    for gc in chips:
+        for t in range(2):
+            r, c = role(gc, t), gc % 2
+            for i in range(2):
+                if r == "R":
+                    blk, s = (t, 1 - c, i), core(gc, b(t, i))
+                    d = core(gc ^ 1, a(t, i))
+                    have[(d, blk)].append(send(MATE, s, have[(s, blk)], d, 32))
+                elif r == "L":
+                    blk, s = (t, c, i), core(gc, b(t, i))
+                    d = core(gc ^ 1, b(t, i))
+                    have[(d, blk)].append(send(MATE, s, have[(s, blk)], d, 32))
+                    blk, s = (t, 1 - c, i), core(gc, a(t, i))
+                    late[(gc, blk)] = send(MATE, s, have[(s, blk)], core(gc, b(t, i)), 32)
+
+    acc, relay = {}, {}
+    for gc in chips:
+        for t in range(2):
+            r, c = role(gc, t), gc % 2
+            for i in range(2):
+                if r == "L":
+                    blk = (t, 1 - c, i)
+                    d = core(gc ^ 1, a(t, i))
+                    have[(d, blk)].append(send(PLANE, core(gc, b(t, i)), [late[(gc, blk)]], d, 32))
+                    continue
+                blk, s = (t, c, i), core(gc, a(t, i))
+                own = owners(group(gc), t, c)
+                for o, (off, w) in zip(own, pieces(len(own), t, i)):
+                    d = core(o, b(t, i))
+                    acc.setdefault((d, blk), [])
+                    if r != "M":
+                        acc[(d, blk)].append(send(PLANE, s, cut(have[(s, blk)], off), d, w))
+                if r in "MC":
+                    blk, s = (t, 1 - c, i), core(gc, b(t, i))
+                    own = owners(group(gc), t, 1 - c)
+                    for o, (off, w) in zip(own, pieces(len(own), t, i)):
+                        d = core(o ^ 1, b(t, i))
+                        relay.setdefault((d, blk), []).append((send(PLANE, s, cut(have[(s, blk)], off), d, w), w))
+    for gc in chips:
+        for t in range(2):
+            if role(gc, t) == "M":
+                for i in range(2):
+                    blk, s = (t, gc % 2, i), core(gc, a(t, i))
+                    own = owners(group(gc), t, gc % 2)
+                    for o, (off, w) in zip(own, pieces(len(own), t, i)):
+                        d = core(o, b(t, i))
+                        acc[(d, blk)].append(send(RELAY, s, cut(have[(s, blk)], off), d, w))
+    for (s, blk), got in sorted(relay.items()):
+        d = s ^ 8
+        acc[(d, blk)].append(send(RELAY, s, [x for x, w in got], d, got[0][1]))
+
+    if n_groups == 2:
+        swapped = {}
+        for blk in blocks:
+            t, p, i = blk
+            o0, o1 = owners(0, t, p), owners(1, t, p)
+            if len(o0) != len(o1):
+                raise ValueError("the hosts have different numbers of owners")
+            for x, y, (off, w) in zip(o0, o1, pieces(len(o0), t, i)):
+                for s, d in ((core(x, b(t, i)), core(y, b(t, i))), (core(y, b(t, i)), core(x, b(t, i)))):
+                    swapped[(d, blk)] = send(HOST, s, acc[(s, blk)], d, w)
+        for k, v in swapped.items():
+            acc[k].append(v)
+
+    for blk in blocks:
+        t, p, i = blk
+        for grp in range(n_groups):
+            own = owners(grp, t, p)
+            for o, (off, w) in zip(own, pieces(len(own), t, i)):
+                dsts = []
+                for gc in chips:
+                    r = role(gc, t)
+                    if group(gc) != grp or r == "L":
+                        continue
+                    if gc % 2 == p or r == "M":
+                        dsts.append((core(gc, b(t, 1 - i)), "res", col(*blk) + off))
+                    elif r == "C":
+                        dsts.append((core(gc, a(t, i)), "res", col(*blk) + off))
+                emit(GATHER, core(o, b(t, i)), acc[(core(o, b(t, i)), blk)], dsts, w)
+
+    def rest(gc, but):
+        return [core(gc, k) for k in range(8) if core(gc, k) not in but]
+
+    def block_to(stage, s, blk, cores):
+        emit(stage, s, [("res", col(*blk))], [(d, "res", col(*blk)) for d in cores], 32)
+
+    for gc in chips:
+        for t in range(2):
+            r, c = role(gc, t), gc % 2
+            for i in range(2):
+                mine, other = (t, c, i), (t, 1 - c, i)
+                sb, sa = core(gc, b(t, 1 - i)), core(gc, a(t, i))
+                if r == "R":
+                    block_to(BACK, sb, mine, rest(gc, [sb]) + [core(gc ^ 1, a(t, i))])
+                    block_to(SPREAD, sa, other, rest(gc, [sa]))
+                elif r == "C":
+                    block_to(BACK, sb, mine, rest(gc, [sb]))
+                    block_to(BACK, sa, other, rest(gc, [sa]))
+                elif r == "M":
+                    block_to(BACK, sb, mine, rest(gc, [sb]) + [core(gc ^ 1, a(t, i))])
+                    block_to(BACK, sb, other, [sa, core(gc ^ 1, b(t, i))])
+                    block_to(SPREAD, sa, other, rest(gc, [sa, sb]))
+                else:
+                    block_to(SPREAD, sa, other, rest(gc, [sa]))
+                    block_to(SPREAD, core(gc, b(t, i)), mine, rest(gc, [core(gc, b(t, i))]))
+
+    n_stages = SPREAD
+    calls = [[[] for s in range(n_stages + 1)] for c in range(N_CORES)]
+    expect = [[0] * (n_stages + 1) for c in range(N_CORES)]
+    sent = [0] * N_CORES
+    bins = {}
+    for op in ops:
+        bins.setdefault((op[1], op[0], op[4]), []).append(op)
+    for (src, stage, w), group_ops in sorted(bins.items()):
+        on_chip = all(d[0] // 8 == src // 8 for op in group_ops for d in op[3])
+        engines = 16 if on_chip else 8
+        n_calls = -(-len(group_ops) // engines)
+        size = -(-len(group_ops) // n_calls)
+        for k in range(0, len(group_ops), size):
+            part = group_ops[k:k + size]
+            e = 1
+            while 2 * e * len(part) <= engines:
+                e *= 2
+            call = []
+            for n, op in enumerate(part):
+                call.append((((1 << e) - 1) << (n * e), e, op[2], op[3], w))
+                sent[src] += e
+                for d in op[3]:
+                    expect[d[0]][stage] += e
+            calls[src][stage].append(call)
+    return calls, expect, sent, max(top), n_stages
+
+
+PLAN_CACHE = {}
+
+
+def plan_for(dead):
+    if "plan" not in PLAN_CACHE:
+        PLAN_CACHE["plan"] = build_plan(dead, BY_HOST)
+    return PLAN_CACHE["plan"]
+
+
+LAND_COLS = 320
+SCRATCH = {
+    "xs": ("sbuf", [128, 256], "float32"),
+    "land": ("sbuf", [128, LAND_COLS], "float32"),
+    "res": ("sbuf", [128, 256], "float32"),
+}
+SEMAPHORES = ["loaded", "stored", "sent", "s1", "s2", "s3", "s4", "s5", "s6", "s7", "s8"]
+
+
+def rank_program(g, core, T, topo):
+    calls, expect, sent, land_cols, n_stages = plan_for(T.tables["DEAD"])
+    if land_cols > LAND_COLS:
+        raise ValueError("land needs %d columns" % land_cols)
+    sems = [None, T.sem.s1, T.sem.s2, T.sem.s3, T.sem.s4, T.sem.s5, T.sem.s6, T.sem.s7, T.sem.s8]
+    bufs = {"xs": T.xs, "land": T.land, "res": T.res}
+
+    g.dma_start(T.xs[:], T.x[:]).then_inc(T.sem.loaded, 16)
+    g.wait_ge(T.sem.loaded, 16)
+    for stage in range(1, n_stages + 1):
+        if stage > 1 and expect[core][stage - 1]:
+            g.wait_ge(sems[stage - 1], expect[core][stage - 1])
+        for call in calls[core][stage]:
+            transfers = []
+            for mask, e, srcs, dsts, w in call:
+                ids = []
+                for d in dsts:
+                    rid, pid = topo.addr(d[0], core)
+                    ids.append(bass.DstId(rid=rid, pnc=pid))
+                transfers.append(bass.RemoteDMATransfer(
+                    dst_ids=ids, dma_engine_mask=mask, remote_sem=sems[stage],
+                    srcs=[bufs[n][:, o:o + w] for n, o in srcs],
+                    dsts=[bufs[d[1]][:, d[2]:d[2] + w] for d in dsts],
+                    alu_op=1 if len(srcs) > 1 else 0))
+            g.remote_dma_fused(transfers, local_sem=T.sem.sent)
+    if expect[core][n_stages]:
+        g.wait_ge(sems[n_stages], expect[core][n_stages])
+    g.dma_start(T.y[:], T.res[:]).then_inc(T.sem.stored, 16)
+    g.wait_ge(T.sem.sent, sent[core])
+    g.wait_ge(T.sem.stored, 16)

@@ -56,10 +56,11 @@ def build_plan(dead, by_host):
     def col(t, p, i):
         return 128 * t + 64 * p + 32 * i
 
-    CHIP, MATE, PLANE, RELAY, HOST = 1, 2, 3, 4, 5
+    CHIP, HEAD, MATE, PLANE, HOST = 1, 2, 3, 4, 5
     GATHER = 6 if by_host else 5
     BACK, SPREAD = GATHER + 1, GATHER + 2
     blocks = [(t, p, i) for t in range(2) for p in range(2) for i in range(2)]
+    sides = [(gc, t, i) for gc in chips for t in range(2) for i in range(2)]
     ops, top = [], [0] * N_CORES
 
     def slot(c, w):
@@ -92,57 +93,49 @@ def build_plan(dead, by_host):
                 if core(gc, k) != h:
                     have[(h, blk)].append(send(CHIP, core(gc, k), [("xs", col(*blk))], h, 32))
 
-    late = {}
-    for gc in chips:
-        for t in range(2):
-            r, c = role(gc, t), gc % 2
-            for i in range(2):
-                if r == "R":
-                    blk, s = (t, 1 - c, i), core(gc, b(t, i))
-                    d = core(gc ^ 1, a(t, i))
-                    have[(d, blk)].append(send(MATE, s, have[(s, blk)], d, 32))
-                elif r == "L":
-                    blk, s = (t, c, i), core(gc, b(t, i))
-                    d = core(gc ^ 1, b(t, i))
-                    have[(d, blk)].append(send(MATE, s, have[(s, blk)], d, 32))
-                    blk, s = (t, 1 - c, i), core(gc, a(t, i))
-                    late[(gc, blk)] = send(MATE, s, have[(s, blk)], core(gc, b(t, i)), 32)
+    late, ride = {}, {}
+    for gc, t, i in sides:
+        r, c = role(gc, t), gc % 2
+        sa, sb = core(gc, a(t, i)), core(gc, b(t, i))
+        if r == "L":
+            have[(sb ^ 8, (t, c, i))].append(send(HEAD, sb, have[(sb, (t, c, i))], sb ^ 8, 32))
+            late[sb] = send(HEAD, sa, have[(sa, (t, 1 - c, i))], sb, 32)
+        elif r == "C":
+            blk, help_ = (t, 1 - c, i), owners(group(gc), t, c)
+            for k in range(2):
+                d = core(help_[-1 - 2 * i - k], b(t, i))
+                ride.setdefault((d, blk), {}).setdefault(k, []).append(send(HEAD, sb, cut(have[(sb, blk)], 16 * k), d, 16))
 
-    acc, relay = {}, {}
-    for gc in chips:
-        for t in range(2):
-            r, c = role(gc, t), gc % 2
-            for i in range(2):
-                if r == "L":
-                    blk = (t, 1 - c, i)
-                    d = core(gc ^ 1, a(t, i))
-                    have[(d, blk)].append(send(PLANE, core(gc, b(t, i)), [late[(gc, blk)]], d, 32))
-                    continue
-                blk, s = (t, c, i), core(gc, a(t, i))
-                own = owners(group(gc), t, c)
-                for o, (off, w) in zip(own, pieces(len(own), t, i)):
-                    d = core(o, b(t, i))
-                    acc.setdefault((d, blk), [])
-                    if r != "M":
-                        acc[(d, blk)].append(send(PLANE, s, cut(have[(s, blk)], off), d, w))
-                if r in "MC":
-                    blk, s = (t, 1 - c, i), core(gc, b(t, i))
-                    own = owners(group(gc), t, 1 - c)
-                    for o, (off, w) in zip(own, pieces(len(own), t, i)):
-                        d = core(o ^ 1, b(t, i))
-                        relay.setdefault((d, blk), []).append((send(PLANE, s, cut(have[(s, blk)], off), d, w), w))
-    for gc in chips:
-        for t in range(2):
-            if role(gc, t) == "M":
-                for i in range(2):
-                    blk, s = (t, gc % 2, i), core(gc, a(t, i))
-                    own = owners(group(gc), t, gc % 2)
-                    for o, (off, w) in zip(own, pieces(len(own), t, i)):
-                        d = core(o, b(t, i))
-                        acc[(d, blk)].append(send(RELAY, s, cut(have[(s, blk)], off), d, w))
+    relay = {}
+    for gc, t, i in sides:
+        r, c = role(gc, t), gc % 2
+        blk, sb = (t, 1 - c, i), core(gc, b(t, i))
+        da = core(gc ^ 1, a(t, i))
+        if r == "R" and (sb, blk) in ride:
+            off = slot(da, 32)
+            for k in range(2):
+                emit(MATE, sb, cut(have[(sb, blk)], 16 * k) + ride[(sb, blk)].get(k, []), [(da, "land", off + 16 * k)], 16)
+            have[(da, blk)].append(("land", off))
+        elif r == "R":
+            have[(da, blk)].append(send(MATE, sb, have[(sb, blk)], da, 32))
+        elif r == "L":
+            have[(da, blk)].append(send(MATE, sb, [late[sb]], da, 32))
+        elif r == "M":
+            own = owners(group(gc), t, 1 - c)
+            for o, (off, w) in zip(own, pieces(len(own), t, i)):
+                d = core(o ^ 1, b(t, i))
+                relay.setdefault((d, blk), []).append((send(MATE, sb, cut(have[(sb, blk)], off), d, w), w))
+
+    acc = {}
+    for gc, t, i in sides:
+        if role(gc, t) != "L":
+            blk, s = (t, gc % 2, i), core(gc, a(t, i))
+            own = owners(group(gc), t, gc % 2)
+            for o, (off, w) in zip(own, pieces(len(own), t, i)):
+                d = core(o, b(t, i))
+                acc.setdefault((d, blk), []).append(send(PLANE, s, cut(have[(s, blk)], off), d, w))
     for (s, blk), got in sorted(relay.items()):
-        d = s ^ 8
-        acc[(d, blk)].append(send(RELAY, s, [x for x, w in got], d, got[0][1]))
+        acc[(s ^ 8, blk)].append(send(PLANE, s, [x for x, w in got], s ^ 8, got[0][1]))
 
     if n_groups == 2:
         swapped = {}
@@ -179,25 +172,26 @@ def build_plan(dead, by_host):
     def block_to(stage, s, blk, cores):
         emit(stage, s, [("res", col(*blk))], [(d, "res", col(*blk)) for d in cores], 32)
 
-    for gc in chips:
-        for t in range(2):
-            r, c = role(gc, t), gc % 2
-            for i in range(2):
-                mine, other = (t, c, i), (t, 1 - c, i)
-                sb, sa = core(gc, b(t, 1 - i)), core(gc, a(t, i))
-                if r == "R":
-                    block_to(BACK, sb, mine, rest(gc, [sb]) + [core(gc ^ 1, a(t, i))])
-                    block_to(SPREAD, sa, other, rest(gc, [sa]))
-                elif r == "C":
-                    block_to(BACK, sb, mine, rest(gc, [sb]))
-                    block_to(BACK, sa, other, rest(gc, [sa]))
-                elif r == "M":
-                    block_to(BACK, sb, mine, rest(gc, [sb]) + [core(gc ^ 1, a(t, i))])
-                    block_to(BACK, sb, other, [sa, core(gc ^ 1, b(t, i))])
-                    block_to(SPREAD, sa, other, rest(gc, [sa, sb]))
-                else:
-                    block_to(SPREAD, sa, other, rest(gc, [sa]))
-                    block_to(SPREAD, core(gc, b(t, i)), mine, rest(gc, [core(gc, b(t, i))]))
+    for gc, t, i in sides:
+        r, c = role(gc, t), gc % 2
+        mine, other = (t, c, i), (t, 1 - c, i)
+        sa, sb, sx = core(gc, a(t, i)), core(gc, b(t, 1 - i)), core(gc, b(t, i))
+        if r == "R":
+            block_to(BACK, sb, mine, rest(gc, [sb, sx]) + [sa ^ 8])
+            block_to(SPREAD, sa, mine, [sx])
+            block_to(SPREAD, sa, other, rest(gc, [sa]))
+        elif r == "C":
+            block_to(BACK, sb, mine, rest(gc, [sb]))
+            block_to(BACK, sa, other, rest(gc, [sa]))
+        elif r == "M":
+            left = [sx, core(gc, a(t, 1 - i))]
+            block_to(BACK, sb, mine, rest(gc, [sb] + left) + [sa ^ 8])
+            block_to(BACK, sb, other, [sa, sx ^ 8])
+            block_to(SPREAD, sa, mine, left)
+            block_to(SPREAD, sa, other, rest(gc, [sa, sb]))
+        else:
+            block_to(SPREAD, sa, other, rest(gc, [sa]))
+            block_to(SPREAD, sx, mine, rest(gc, [sx]))
 
     n_stages = SPREAD
     calls = [[[] for s in range(n_stages + 1)] for c in range(N_CORES)]
@@ -235,7 +229,7 @@ def plan_for(dead):
     return PLAN_CACHE["plan"]
 
 
-LAND_COLS = 320
+LAND_COLS = 296
 SCRATCH = {
     "xs": ("sbuf", [128, 256], "float32"),
     "land": ("sbuf", [128, LAND_COLS], "float32"),

@@ -2,10 +2,9 @@ import comms_topo
 import concourse.bass as bass
 
 N_CORES = 256
-BY_HOST = True
 
 
-def build_plan(dead, by_host):
+def build_plan(dead):
     if dead["chips"]:
         raise ValueError("missing chips are not planned for")
     dead_ports = set((c, d) for c, d in dead["switch_ports"])
@@ -26,13 +25,11 @@ def build_plan(dead, by_host):
             return "M" if mine else "L"
         raise ValueError("chip %d side %d is cut off" % (gc, t))
 
-    def group(gc):
-        return gc // 16 if by_host else 0
+    def host(gc):
+        return gc // 16
 
-    n_groups = 2 if by_host else 1
-
-    def owners(grp, t, p):
-        return [c for c in chips if group(c) == grp and c % 2 == p and role(c, t) == "R"]
+    def owners(h, t, p):
+        return [c for c in chips if host(c) == h and c % 2 == p and role(c, t) == "R"]
 
     def pieces(n, t, i):
         base, extra = 32 // n, 32 % n
@@ -56,9 +53,7 @@ def build_plan(dead, by_host):
     def col(t, p, i):
         return 128 * t + 64 * p + 32 * i
 
-    CHIP, HEAD, MATE, PLANE, HOST = 1, 2, 3, 4, 5
-    GATHER = 6 if by_host else 5
-    BACK, SPREAD = GATHER + 1, GATHER + 2
+    CHIP, HEAD, MATE, PLANE, HOST, GATHER, BACK, SPREAD = 1, 2, 3, 4, 5, 6, 7, 8
     blocks = [(t, p, i) for t in range(2) for p in range(2) for i in range(2)]
     sides = [(gc, t, i) for gc in chips for t in range(2) for i in range(2)]
     ops, top = [], [0] * N_CORES
@@ -101,9 +96,9 @@ def build_plan(dead, by_host):
             have[(sb ^ 8, (t, c, i))].append(send(HEAD, sb, have[(sb, (t, c, i))], sb ^ 8, 32))
             late[sb] = send(HEAD, sa, have[(sa, (t, 1 - c, i))], sb, 32)
         elif r == "C":
-            blk, help_ = (t, 1 - c, i), owners(group(gc), t, c)
+            blk, helpers = (t, 1 - c, i), owners(host(gc), t, c)
             for k in range(2):
-                d = core(help_[-1 - 2 * i - k], b(t, i))
+                d = core(helpers[-1 - 2 * i - k], b(t, i))
                 ride.setdefault((d, blk), {}).setdefault(k, []).append(send(HEAD, sb, cut(have[(sb, blk)], 16 * k), d, 16))
 
     relay = {}
@@ -121,7 +116,7 @@ def build_plan(dead, by_host):
         elif r == "L":
             have[(da, blk)].append(send(MATE, sb, [late[sb]], da, 32))
         elif r == "M":
-            own = owners(group(gc), t, 1 - c)
+            own = owners(host(gc), t, 1 - c)
             for o, (off, w) in zip(own, pieces(len(own), t, i)):
                 d = core(o ^ 1, b(t, i))
                 relay.setdefault((d, blk), []).append((send(MATE, sb, cut(have[(sb, blk)], off), d, w), w))
@@ -130,35 +125,34 @@ def build_plan(dead, by_host):
     for gc, t, i in sides:
         if role(gc, t) != "L":
             blk, s = (t, gc % 2, i), core(gc, a(t, i))
-            own = owners(group(gc), t, gc % 2)
+            own = owners(host(gc), t, gc % 2)
             for o, (off, w) in zip(own, pieces(len(own), t, i)):
                 d = core(o, b(t, i))
                 acc.setdefault((d, blk), []).append(send(PLANE, s, cut(have[(s, blk)], off), d, w))
     for (s, blk), got in sorted(relay.items()):
         acc[(s ^ 8, blk)].append(send(PLANE, s, [x for x, w in got], s ^ 8, got[0][1]))
 
-    if n_groups == 2:
-        swapped = {}
-        for blk in blocks:
-            t, p, i = blk
-            o0, o1 = owners(0, t, p), owners(1, t, p)
-            if len(o0) != len(o1):
-                raise ValueError("the hosts have different numbers of owners")
-            for x, y, (off, w) in zip(o0, o1, pieces(len(o0), t, i)):
-                for s, d in ((core(x, b(t, i)), core(y, b(t, i))), (core(y, b(t, i)), core(x, b(t, i)))):
-                    swapped[(d, blk)] = send(HOST, s, acc[(s, blk)], d, w)
-        for k, v in swapped.items():
-            acc[k].append(v)
+    swapped = {}
+    for blk in blocks:
+        t, p, i = blk
+        o0, o1 = owners(0, t, p), owners(1, t, p)
+        if len(o0) != len(o1):
+            raise ValueError("the hosts have different numbers of owners")
+        for x, y, (off, w) in zip(o0, o1, pieces(len(o0), t, i)):
+            for s, d in ((core(x, b(t, i)), core(y, b(t, i))), (core(y, b(t, i)), core(x, b(t, i)))):
+                swapped[(d, blk)] = send(HOST, s, acc[(s, blk)], d, w)
+    for k, v in swapped.items():
+        acc[k].append(v)
 
     for blk in blocks:
         t, p, i = blk
-        for grp in range(n_groups):
-            own = owners(grp, t, p)
+        for h in range(2):
+            own = owners(h, t, p)
             for o, (off, w) in zip(own, pieces(len(own), t, i)):
                 dsts = []
                 for gc in chips:
                     r = role(gc, t)
-                    if group(gc) != grp or r == "L":
+                    if host(gc) != h or r == "L":
                         continue
                     if gc % 2 == p or r == "M":
                         dsts.append((core(gc, b(t, 1 - i)), "res", col(*blk) + off))
@@ -225,11 +219,11 @@ PLAN_CACHE = {}
 
 def plan_for(dead):
     if "plan" not in PLAN_CACHE:
-        PLAN_CACHE["plan"] = build_plan(dead, BY_HOST)
+        PLAN_CACHE["plan"] = build_plan(dead)
     return PLAN_CACHE["plan"]
 
 
-LAND_COLS = 296
+LAND_COLS = 276
 SCRATCH = {
     "xs": ("sbuf", [128, 256], "float32"),
     "land": ("sbuf", [128, LAND_COLS], "float32"),

import comms_topo
import concourse.bass as bass

N_CORES = 256


def build_plan(dead):
    if dead["chips"]:
        raise ValueError("missing chips are not planned for")
    dead_ports = set((c, d) for c, d in dead["switch_ports"])
    dead_mates = set()
    for c, d in dead["mate_links"]:
        dead_mates.add((c, d))
        dead_mates.add((c ^ 1, d))
    side_die = [comms_topo.die(0), comms_topo.die(4)]
    chips = list(range(N_CORES // 8))

    def role(gc, t):
        d = side_die[t]
        mine, other = (gc, d) not in dead_ports, (gc ^ 1, d) not in dead_ports
        link = (gc, d) not in dead_mates
        if mine and other:
            return "R" if link else "C"
        if link and (mine or other):
            return "M" if mine else "L"
        raise ValueError("chip %d side %d is cut off" % (gc, t))

    def host(gc):
        return gc // 16

    def owners(h, t, p):
        return [c for c in chips if host(c) == h and c % 2 == p and role(c, t) == "R"]

    def pieces(n, t, i):
        base, extra = 32 // n, 32 % n
        first = (extra * (2 * t + i)) % n
        out, off = [], 0
        for j in range(n):
            w = base + (1 if (j - first) % n < extra else 0)
            out.append((off, w))
            off += w
        return out

    def core(gc, k):
        return 8 * gc + k

    def a(t, i):
        return 4 * t + i

    def b(t, i):
        return 4 * t + 2 + i

    def col(t, p, i):
        return 128 * t + 64 * p + 32 * i

    CHIP, HEAD, MATE, PLANE, HOST, GATHER, BACK, SPREAD = 1, 2, 3, 4, 5, 6, 7, 8
    blocks = [(t, p, i) for t in range(2) for p in range(2) for i in range(2)]
    sides = [(gc, t, i) for gc in chips for t in range(2) for i in range(2)]
    ops, top = [], [0] * N_CORES

    def slot(c, w):
        off = top[c]
        top[c] += w
        return off

    def emit(stage, src, srcs, dsts, w):
        for k in range(0, len(dsts), 16):
            ops.append((stage, src, tuple(srcs), tuple(dsts[k:k + 16]), w))

    def send(stage, src, srcs, dst, w):
        off = slot(dst, w)
        emit(stage, src, srcs, [(dst, "land", off)], w)
        return ("land", off)

    def cut(bufs, off):
        return [(n, o + off) for n, o in bufs]

    have = {}
    for gc in chips:
        for blk in blocks:
            t, p, i = blk
            own = p == gc % 2
            if role(gc, t) == "L":
                own = not own
            h = core(gc, a(t, i) if own else b(t, i))
            have[(h, blk)] = [("xs", col(*blk))]
            for k in range(8):
                if core(gc, k) != h:
                    have[(h, blk)].append(send(CHIP, core(gc, k), [("xs", col(*blk))], h, 32))

    late, ride = {}, {}
    for gc, t, i in sides:
        r, c = role(gc, t), gc % 2
        sa, sb = core(gc, a(t, i)), core(gc, b(t, i))
        if r == "L":
            have[(sb ^ 8, (t, c, i))].append(send(HEAD, sb, have[(sb, (t, c, i))], sb ^ 8, 32))
            late[sb] = send(HEAD, sa, have[(sa, (t, 1 - c, i))], sb, 32)
        elif r == "C":
            blk, helpers = (t, 1 - c, i), owners(host(gc), t, c)
            for k in range(2):
                d = core(helpers[-1 - 2 * i - k], b(t, i))
                ride.setdefault((d, blk), {}).setdefault(k, []).append(send(HEAD, sb, cut(have[(sb, blk)], 16 * k), d, 16))

    relay = {}
    for gc, t, i in sides:
        r, c = role(gc, t), gc % 2
        blk, sb = (t, 1 - c, i), core(gc, b(t, i))
        da = core(gc ^ 1, a(t, i))
        if r == "R" and (sb, blk) in ride:
            off = slot(da, 32)
            for k in range(2):
                emit(MATE, sb, cut(have[(sb, blk)], 16 * k) + ride[(sb, blk)].get(k, []), [(da, "land", off + 16 * k)], 16)
            have[(da, blk)].append(("land", off))
        elif r == "R":
            have[(da, blk)].append(send(MATE, sb, have[(sb, blk)], da, 32))
        elif r == "L":
            have[(da, blk)].append(send(MATE, sb, [late[sb]], da, 32))
        elif r == "M":
            own = owners(host(gc), t, 1 - c)
            for o, (off, w) in zip(own, pieces(len(own), t, i)):
                d = core(o ^ 1, b(t, i))
                relay.setdefault((d, blk), []).append((send(MATE, sb, cut(have[(sb, blk)], off), d, w), w))

    acc = {}
    for gc, t, i in sides:
        if role(gc, t) != "L":
            blk, s = (t, gc % 2, i), core(gc, a(t, i))
            own = owners(host(gc), t, gc % 2)
            for o, (off, w) in zip(own, pieces(len(own), t, i)):
                d = core(o, b(t, i))
                acc.setdefault((d, blk), []).append(send(PLANE, s, cut(have[(s, blk)], off), d, w))
    for (s, blk), got in sorted(relay.items()):
        acc[(s ^ 8, blk)].append(send(PLANE, s, [x for x, w in got], s ^ 8, got[0][1]))

    swapped = {}
    for blk in blocks:
        t, p, i = blk
        o0, o1 = owners(0, t, p), owners(1, t, p)
        if len(o0) != len(o1):
            raise ValueError("the hosts have different numbers of owners")
        for x, y, (off, w) in zip(o0, o1, pieces(len(o0), t, i)):
            for s, d in ((core(x, b(t, i)), core(y, b(t, i))), (core(y, b(t, i)), core(x, b(t, i)))):
                swapped[(d, blk)] = send(HOST, s, acc[(s, blk)], d, w)
    for k, v in swapped.items():
        acc[k].append(v)

    for blk in blocks:
        t, p, i = blk
        for h in range(2):
            own = owners(h, t, p)
            for o, (off, w) in zip(own, pieces(len(own), t, i)):
                dsts = []
                for gc in chips:
                    r = role(gc, t)
                    if host(gc) != h or r == "L":
                        continue
                    if gc % 2 == p or r == "M":
                        dsts.append((core(gc, b(t, 1 - i)), "res", col(*blk) + off))
                    elif r == "C":
                        dsts.append((core(gc, a(t, i)), "res", col(*blk) + off))
                emit(GATHER, core(o, b(t, i)), acc[(core(o, b(t, i)), blk)], dsts, w)

    def rest(gc, but):
        return [core(gc, k) for k in range(8) if core(gc, k) not in but]

    def block_to(stage, s, blk, cores):
        emit(stage, s, [("res", col(*blk))], [(d, "res", col(*blk)) for d in cores], 32)

    for gc, t, i in sides:
        r, c = role(gc, t), gc % 2
        mine, other = (t, c, i), (t, 1 - c, i)
        sa, sb, sx = core(gc, a(t, i)), core(gc, b(t, 1 - i)), core(gc, b(t, i))
        if r == "R":
            block_to(BACK, sb, mine, rest(gc, [sb, sx]) + [sa ^ 8])
            block_to(SPREAD, sa, mine, [sx])
            block_to(SPREAD, sa, other, rest(gc, [sa]))
        elif r == "C":
            block_to(BACK, sb, mine, rest(gc, [sb]))
            block_to(BACK, sa, other, rest(gc, [sa]))
        elif r == "M":
            left = [sx, core(gc, a(t, 1 - i))]
            block_to(BACK, sb, mine, rest(gc, [sb] + left) + [sa ^ 8])
            block_to(BACK, sb, other, [sa, sx ^ 8])
            block_to(SPREAD, sa, mine, left)
            block_to(SPREAD, sa, other, rest(gc, [sa, sb]))
        else:
            block_to(SPREAD, sa, other, rest(gc, [sa]))
            block_to(SPREAD, sx, mine, rest(gc, [sx]))

    n_stages = SPREAD
    calls = [[[] for s in range(n_stages + 1)] for c in range(N_CORES)]
    expect = [[0] * (n_stages + 1) for c in range(N_CORES)]
    sent = [0] * N_CORES
    bins = {}
    for op in ops:
        bins.setdefault((op[1], op[0], op[4]), []).append(op)
    for (src, stage, w), group_ops in sorted(bins.items()):
        on_chip = all(d[0] // 8 == src // 8 for op in group_ops for d in op[3])
        engines = 16 if on_chip else 8
        n_calls = -(-len(group_ops) // engines)
        size = -(-len(group_ops) // n_calls)
        for k in range(0, len(group_ops), size):
            part = group_ops[k:k + size]
            e = 1
            while 2 * e * len(part) <= engines:
                e *= 2
            call = []
            for n, op in enumerate(part):
                call.append((((1 << e) - 1) << (n * e), e, op[2], op[3], w))
                sent[src] += e
                for d in op[3]:
                    expect[d[0]][stage] += e
            calls[src][stage].append(call)
    return calls, expect, sent, max(top), n_stages


PLAN_CACHE = {}


def plan_for(dead):
    if "plan" not in PLAN_CACHE:
        PLAN_CACHE["plan"] = build_plan(dead)
    return PLAN_CACHE["plan"]


LAND_COLS = 276
SCRATCH = {
    "xs": ("sbuf", [128, 256], "float32"),
    "land": ("sbuf", [128, LAND_COLS], "float32"),
    "res": ("sbuf", [128, 256], "float32"),
}
SEMAPHORES = ["loaded", "stored", "sent", "s1", "s2", "s3", "s4", "s5", "s6", "s7", "s8"]


def rank_program(g, core, T, topo):
    calls, expect, sent, land_cols, n_stages = plan_for(T.tables["DEAD"])
    if land_cols > LAND_COLS:
        raise ValueError("land needs %d columns" % land_cols)
    sems = [None, T.sem.s1, T.sem.s2, T.sem.s3, T.sem.s4, T.sem.s5, T.sem.s6, T.sem.s7, T.sem.s8]
    bufs = {"xs": T.xs, "land": T.land, "res": T.res}

    g.dma_start(T.xs[:], T.x[:]).then_inc(T.sem.loaded, 16)
    g.wait_ge(T.sem.loaded, 16)
    for stage in range(1, n_stages + 1):
        if stage > 1 and expect[core][stage - 1]:
            g.wait_ge(sems[stage - 1], expect[core][stage - 1])
        for call in calls[core][stage]:
            transfers = []
            for mask, e, srcs, dsts, w in call:
                ids = []
                for d in dsts:
                    rid, pid = topo.addr(d[0], core)
                    ids.append(bass.DstId(rid=rid, pnc=pid))
                transfers.append(bass.RemoteDMATransfer(
                    dst_ids=ids, dma_engine_mask=mask, remote_sem=sems[stage],
                    srcs=[bufs[n][:, o:o + w] for n, o in srcs],
                    dsts=[bufs[d[1]][:, d[2]:d[2] + w] for d in dsts],
                    alu_op=1 if len(srcs) > 1 else 0))
            g.remote_dma_fused(transfers, local_sem=T.sem.sent)
    if expect[core][n_stages]:
        g.wait_ge(sems[n_stages], expect[core][n_stages])
    g.dma_start(T.y[:], T.res[:]).then_inc(T.sem.stored, 16)
    g.wait_ge(T.sem.sent, sent[core])
    g.wait_ge(T.sem.stored, 16)
